import numpy as np, ml_dtypes
CORES = [35,38,43,46]
N = 4
BF = ml_dtypes.bfloat16
def gentries(a):
    return np.ascontiguousarray(a.reshape(8, 16, -1).transpose(0, 2, 1)).reshape(8, -1)
def gtable(e):
    e = np.asarray(e); return np.ascontiguousarray(e.reshape(8, -1, 16).transpose(0, 2, 1)).reshape(128, -1).astype(np.int32)
V, B, BITS, RO = 2048, 512, 12, 5
M = N * B
W = M + V - B
C = 2 ** BITS
def seen(q, p):
    bq = np.ascontiguousarray(q[..., :B].transpose(1, 2, 0, 3)).reshape(8, 16, M)
    bp = np.ascontiguousarray(p[..., :B].transpose(1, 0, 2)).reshape(8, M)
    gs, qps, qgs = [], [], []
    for a in range(N):
        wq = np.concatenate([bq, q[a, :, :, B:]], axis=2); wp = np.concatenate([bp, p[a, :, B:]], axis=1)
        g = np.take_along_axis(wp, p[a], 1)
        gs.append(g); qps.append(np.take_along_axis(wq, p[a][:, None, :], 2)); qgs.append(np.take_along_axis(wq, g[:, None, :], 2))
    return np.stack(gs), np.stack(qps), np.stack(qgs)
def dots(am, z):
    return np.matmul(am.transpose(0, 1, 3, 2), z)
def codes(am, t, z):
    return np.add.reduce(np.where(dots(am, z)[:, :, :BITS] > t[:, :, :BITS], 2 ** np.arange(BITS)[:, None], 0), axis=2)
def forest(rng):
    span = rng.choice(np.array([2, 16, B, M]), (8, 1)); i = np.arange(M)
    o = np.argsort(rng.random((8, M)), axis=1); back = np.minimum(i, (rng.random((8, M)) * span).astype(np.int64) + 1)
    pb = np.zeros((8, M), np.int64); np.put_along_axis(pb, o, np.take_along_axis(o, i - np.where(rng.random((8, M)) < 0.02, 0, back), 1), 1)
    h = V - B; i = np.arange(h); span = rng.choice(np.array([2, 16, B, h]), (N, 8, 1))
    o = np.argsort(rng.random((N, 8, h)), axis=2); back = np.minimum(i, (rng.random((N, 8, h)) * span).astype(np.int64) + 1)
    pi = np.zeros((N, 8, h), np.int64); np.put_along_axis(pi, o, np.take_along_axis(o, i - np.where(rng.random((N, 8, h)) < 0.02, 0, back), 2), 2)
    pi = np.where(rng.random((N, 8, h)) < 0.5, rng.integers(0, M, (N, 8, h)), M + pi)
    return np.concatenate([pb.reshape(8, N, B).transpose(1, 0, 2), pi], axis=2)
def parts(rng):
    amp = rng.choice(np.array([8, 24, 64]), (N, 8, 1, V))
    q = 64 + np.floor((2 * rng.random((N, 8, 16, V)) - 1) * amp).astype(np.int64); q = np.clip(q, 0, 127)
    am = rng.integers(-1, 2, (N, 8, 16, 16))
    t = 128 * np.add.reduce(am, axis=2)[..., None] + rng.integers(-30, 31, (N, 8, 16, 1))
    c = np.clip(rng.choice(np.array([0, 8, 24, 64, 111]), (N, 8, 1, C)) + rng.integers(0, 17, (N, 8, 16, C)), 0, 127)
    return q, forest(rng), am, t, c
def pack(q, p, am, t, c):
    big = np.zeros((N, 128, 128), np.float32)
    for h in range(8): big[:, 16 * h:16 * h + 16, 16 * h:16 * h + 16] = am[:, h]
    return {"q": np.ascontiguousarray(q).reshape(N, 128, V).astype(np.float32).astype(BF), "par": np.stack([gtable(a) for a in p]), "amat": big.astype(BF),
            "clr": np.ascontiguousarray(c).reshape(N, 128, C).astype(np.float32).astype(BF), "th": np.ascontiguousarray(t).reshape(N, 128, 1).astype(np.int32)}
def setup_inputs(rng):
    return pack(*parts(rng))
def setup_inputs_edge(rng):
    q, p, am, t, c = parts(rng); q = 64 + rng.integers(-6, 7, q.shape)
    g, qp, qg = seen(q, p); s = dots(am, q + qg); low = rng.integers(0, 2, (N, 8, 16, 1)); low[:, :, 0] = 0; low[:, :, 1] = 1
    t = np.take_along_axis(s, rng.integers(0, V, (N, 8, 16, 1)), 3) - low
    code = codes(am, t, q + qg); gap = np.abs(q - qg)
    for a in range(N):
        for h in range(8):
            w = np.full(C, -1); w[code[a, h]] = np.arange(V); k = np.nonzero(w >= 0)[0]; n = np.arange(len(k))
            e = gap[a, h][:, w[k]].copy(); x = np.argmax(e, axis=0)
            e[x, n] = e[x, n] - ((rng.random(len(k)) < 0.5) & (e[x, n] > 0)).astype(np.int64)
            c[a, h][:, k] = e
    return pack(q, p, am, t, c)
def setup_inputs_chain(rng):
    q, p, am, t, c = parts(rng); k = np.arange(B)
    for r in range(N):
        p[r, 0::2, :B] = (r + 1) % N * B + (k + (r == N - 1)) % B
        p[r, 1::2, :B] = (r - 1) * B + k if r else np.where(k > 0, (N - 1) * B + k - 1, 0)
        p[r, :, B:] = M + np.arange(V - B) - 1; p[r, :, B] = r * B + B - 1
    c[:, 0:2] = 127; c[:, 2:4] = 0
    return pack(q, p, am, t, c)
def setup_inputs_alike(rng):
    q, p, am, t, c = parts(rng)
    p[:, 0:2, :B] = rng.choice(np.array([0, B - 1, B, M - 1]), (N, 2, B)); p[:, 0:2, B:] = rng.choice(np.array([0, M - 1, M, W - 1]), (N, 2, V - B))
    for r in range(N):
        p[r, 2, :B] = r * B + np.arange(B); p[r, 2, B:] = M + np.arange(V - B)
    p[:, 3, B:] = rng.integers(M, W, (N, V - B)); p[:, 4, B:] = rng.integers(0, M, (N, V - B))
    t[:, 5] = -4096; c[:, 5, :, C - 1] = rng.integers(20, 60, (N, 16)); t[:, 6] = 4096; c[:, 6, :, 0] = rng.integers(20, 60, (N, 16))
    q[:, 7] = 127 * rng.integers(0, 2, (N, 16, V)); one = np.arange(16)[:, None] == rng.integers(0, 16, (N, 1, C))
    c[:, 7] = 127 - (one & (rng.random((N, 1, C)) < 0.7)).astype(np.int64)
    return pack(q, p, am, t, c)
def setup_inputs_spread(rng):
    q, p, am, t, c = parts(rng)
    q = np.clip(np.floor(np.exp2(7.5 * rng.random((N, 8, 1, V))) * rng.random((N, 8, 16, V))).astype(np.int64), 0, 127)
    am = am * (rng.random((N, 8, 16, 16)) < rng.choice(np.array([0.1, 0.4, 1.0]), (N, 8, 1, 16)))
    t = np.floor(np.exp2(12 * rng.random((N, 8, 16, 1)) ** 1.5)).astype(np.int64) * rng.choice(np.array([-1, 1]), (N, 8, 16, 1)); t = np.clip(t, -4096, 4096)
    c = np.clip(np.floor(np.exp2(8 * rng.random((N, 8, 1, C))) * (0.5 + rng.random((N, 8, 16, C)))).astype(np.int64), 0, 127)
    return pack(q, p, am, t, c)
def setup_inputs_large(rng):
    q, p, am, t, c = parts(rng)
    q[:, :5] = 127 - np.floor(rng.random((N, 5, 16, V)) * rng.choice(np.array([1, 4, 16, 40]), (N, 5, 1, V))).astype(np.int64)
    cut = rng.integers(0, 3, (N, 5, 1, 16)); cut[:, 4] = 4; less = -rng.integers(0, 2, (N, 5, 16, 16)); less[:, 4] = -1
    sign = rng.choice(np.array([-1, 1]), (N, 5, 1, 16)); sign[:, 0] = 1; sign[:, 1] = -1
    am[:, :5] = sign * np.where(np.argsort(rng.random((N, 5, 16, 16)), axis=2) < cut, less, 1)
    for h in range(5, 8):
        a = int(rng.integers(0, N)); b = (a + 1) % N; ka = int(rng.integers(0, B)); kb = int(rng.integers(0, B))
        p[:, h] = a * B + ka; p[a, h, ka] = b * B + kb; p[b, h, kb] = b * B + kb
        am[:, h] = np.eye(16, dtype=np.int64); mid = rng.integers(32, 96, (N, 16, 1))
        for r in range(N):
            w = rng.permutation(np.concatenate([np.arange(C), rng.integers(0, C, max(V - C, 0))]))[:V]
            bit = (w[None, :] >> np.arange(16)[:, None]) & 1; bit[BITS:] = rng.integers(0, 2, (16 - BITS, V)); u = rng.random((16, V))
            q[r, h] = np.where(bit == 1, mid[r] + 1 + np.floor(u * (127 - mid[r])).astype(np.int64), np.floor(u * (mid[r] + 1)).astype(np.int64))
        t[:, h] = mid + q[b, h, :, kb][None, :, None]
    g, qp, qg = seen(q, p); s = np.take_along_axis(dots(am, q + qg), rng.integers(0, V, (N, 8, 16, 1)), 3)
    low = np.where((s & 3) == 1, 1, np.where((s & 3) == 3, 0, rng.integers(0, 2, s.shape)))
    t[:, :5] = (s - low)[:, :5]
    c[:] = 127 * rng.integers(0, 2, (N, 8, 1, C))
    return pack(q, p, am, t, c)
def check_inputs(d):
    bad = []
    for k in ("q", "clr"):
        x = np.asarray(d[k]).astype(np.float32)
        if not np.all((x >= 0) & (x <= 127) & (x == np.floor(x))): bad.append("numbers of " + k)
    if np.min(d["th"]) < -4096 or np.max(d["th"]) > 4096: bad.append("range of th")
    x = np.asarray(d["amat"]).astype(np.float32); same = np.arange(128)[:, None] // 16 == np.arange(128)[None, :] // 16
    if not np.all((x == 0) | (same & ((x == 1) | (x == -1)))): bad.append("numbers of amat")
    if np.min(d["par"]) < 0 or np.max(d["par"]) > W - 1: bad.append("range of par")
    if np.max(np.stack([gentries(a) for a in d["par"]])[:, :, :B]) > M - 1: bad.append("parents of border columns")
    return bad
def reference(q, par, amat, clr, th):
    x = q.astype(np.float32).astype(np.int64).reshape(N, 8, 16, V); p = np.stack([gentries(a) for a in par]).astype(np.int64)
    big = amat.astype(np.float32).astype(np.int64); am = np.stack([big[:, 16 * h:16 * h + 16, 16 * h:16 * h + 16] for h in range(8)], axis=1)
    c = clr.astype(np.float32).astype(np.int64).reshape(N, 8, 16, C); t = th.astype(np.int64).reshape(N, 8, 16, 1)
    for rnd in range(RO):
        g, xp, xg = seen(x, p)
        code = codes(am, t, x + xg)
        room = np.take_along_axis(c, code[:, :, None, :], 3)
        ok = np.all(room >= np.abs(x - xg), axis=2)
        p = np.where(ok, g, p); x = np.where(ok[:, :, None, :], x, (x + xp) >> 1)
    return {"yq": x.reshape(N, 128, V).astype(np.float32).astype(BF), "yp": np.stack([gtable(a) for a in p]).astype(np.float32)}

@@ -1,0 +1,399 @@
+from concourse.bass import DstId, RemoteDMATransfer
+from concourse.mybir import AluOpType, ActivationFunctionType
+
+N, V, B, RO = 4, 2048, 512, 5
+M = N * B
+W = M + V - B
+CH = [(0, 512, 256), (512, 1280, 384), (1280, 2048, 384)]
+
+SCRATCH = {}
+_BF, _F32, _I32, _U16 = "bfloat16", "float32", "int32", "uint16"
+for _nm, _n, _d in (
+        [(x, 128, _I32) for x in ("parI", "hiI", "loI")] + [(x, 128, _BF) for x in ("hib", "lob", "am", "am2")]
+        + [(x, V, _BF) for x in ("qraw", "yout")] + [("clrs", 4096, _BF), ("ones", 16, _BF), ("yb", 16 + 2048, _BF)]
+        + [(x, 144, _BF) for x in ("z", "zn", "zc")] + [(x, 1, _I32) for x in ("thI", "pI", "pmI")]
+        + [(x, 1, _F32) for x in ("thf", "thr", "pm", "pd", "wn")] + [("bias", 8, _F32), ("rowg", 8, _F32)]
+        + [(x, 16, _F32) for x in ("row", "oh", "pw", "pwo")] + [(x, 128, _F32) for x in ("own0", "own")]
+        + [("Q%d" % k, W, _BF) for k in range(RO + 1)] + [("nf%d" % k, 128, _F32) for k in range(RO + 1)]
+        + [("nw%d" % k, W, _BF) for k in range(RO)] + [("n16_%d" % k, 128, _U16) for k in range(RO)]
+        + [("%s%d" % (x, k), V, _BF) for k in range(2) for x in ("hb", "bits", "okb", "e", "ae")]
+        + [("ah%d" % k, V, "float16") for k in range(2)]
+        + [("%s%d" % (x, k), 128, _F32) for k in range(2) for x in ("dn", "dh", "okm", "t", "t2")]
+        + [("%s%d" % (x, k), 128, _U16) for k in range(2) for x in ("h16_", "c16_")]
+        + [("l34_%d" % k, 256, _F32) for k in range(2)] + [("l16_%d" % k, 256, _U16) for k in range(2)]):
+    SCRATCH[_nm] = ("sbuf", [128, _n], _d)
+for _k in range(8):
+    SCRATCH["ps%d" % _k] = ("psum", [128, 512], "float32")
+SEMAPHORES = ["sv", "sa", "sp", "sg", "ls"] + ["%s%d" % (x, k) for x in ("an", "aq") for k in range(RO)] \
+    + ["%s%d" % (x, k) for x in ("ld", "st") for k in range(8)]
+
+CYC, WAKE, GF = 0.83, 90.0, 1.56
+QSEM = {"v": "sv", "a": "sa", "p": "sp", "g": "sg"}
+
+
+def add(G, q, cost, reads, writes, fn, kind="c", sem=None, val=0, deps=()):
+    i = len(G["ops"])
+    edges = {d: True for d in deps}
+    for kindrw, regs in ((0, reads), (1, writes)):
+        for (nm, c0, c1) in regs:
+            psum = nm[:2] == "ps"
+            if psum:
+                c0, c1 = 0, 512
+            for (a0, a1, o, w) in G["hist"].setdefault(nm, []):
+                if o == i or a0 >= c1 or c0 >= a1:
+                    continue
+                if w and not kindrw:
+                    edges[o] = True
+                elif kindrw or (psum and G["ops"][o]["q"] != q):
+                    edges.setdefault(o, False)
+    for kindrw, regs in ((0, reads), (1, writes)):
+        for (nm, c0, c1) in regs:
+            if nm[:2] == "ps":
+                c0, c1 = 0, 512
+            h = G["hist"][nm]
+            if kindrw:
+                h[:] = [x for x in h if not (x[0] >= c0 and x[1] <= c1)]
+            h.append((c0, c1, i, kindrw))
+    G["ops"].append({"q": q, "cost": cost, "fn": fn, "kind": kind, "sem": sem, "val": val, "edges": edges})
+    return i
+
+
+def schedule(ops):
+    n = len(ops)
+    succ = [[] for _ in range(n)]
+    for i, o in enumerate(ops):
+        for d in o["edges"]:
+            succ[d].append(i)
+    pri = [0.0] * n
+    for i in range(n - 1, -1, -1):
+        pri[i] = ops[i]["cost"] + max([pri[s] + (WAKE if ops[s]["q"] != ops[i]["q"] else 20.0) for s in succ[i]] or [0.0])
+    left = [len(o["edges"]) for o in ops]
+    ready, free = {}, {}
+    rt, start, fin = [0.0] * n, [0.0] * n, [0.0] * n
+    for i in range(n):
+        if left[i] == 0:
+            ready.setdefault(ops[i]["q"], []).append(i)
+    for _ in range(n):
+        best = None
+        for q, lst in ready.items():
+            if not lst:
+                continue
+            if q == "n":
+                c = min(lst, key=lambda i: rt[i])
+                s = rt[c]
+            else:
+                s = max(free.get(q, 0.0), min(rt[i] for i in lst))
+                c = max((i for i in lst if rt[i] <= s + 1e-9), key=lambda i: pri[i])
+            if best is None or s < best[0]:
+                best = (s, q, c)
+        s, q, c = best
+        ready[q].remove(c)
+        start[c], fin[c] = s, s + ops[c]["cost"]
+        free[q] = s + (60.0 if ops[c]["kind"] == "d" else ops[c]["cost"])
+        for x in succ[c]:
+            rt[x] = max(rt[x], fin[c] + (WAKE if ops[x]["q"] != q else 20.0))
+            left[x] -= 1
+            if left[x] == 0:
+                ready.setdefault(ops[x]["q"], []).append(x)
+    return start, fin
+
+
+def build(g, core, T, topo):
+    A, F = AluOpType, ActivationFunctionType
+    r = T.rank_of(core)
+    G = {"ops": [], "hist": {}}
+    X = lambda nm, a, b, s=1: T[nm][:, a:b] if s == 1 else T[nm][:, a:b:s]
+    Y = lambda s: X(*s) if isinstance(s, tuple) else s
+
+    def ts(out, in0, s1, op0, s2=None, op1=None, fast=False):
+        def fn():
+            if op1 is None:
+                return g.vector.tensor_scalar(X(*out), X(*in0), Y(s1), None, op0)
+            return g.vector.tensor_scalar(X(*out), X(*in0), Y(s1), Y(s2), op0, op1)
+        rd = [in0] + [s for s in (s1, s2) if isinstance(s, tuple)]
+        return add(G, "v", max(64.0, (in0[2] - in0[1]) * (0.5 if fast else 1.0)) * CYC, rd, [out[:3]], fn)
+
+    def tt(out, in0, in1, op):
+        cost = max(64.0, (in0[2] - in0[1]) * (1.0 if in0[0][:2] == "ps" else 2.0)) * CYC
+        return add(G, "v", cost, [in0, in1], [out], lambda: g.vector.tensor_tensor(X(*out), X(*in0), X(*in1), op))
+
+    def tc(out, in0):
+        return add(G, "v", max(64.0, in0[2] - in0[1]) * CYC, [in0], [out], lambda: g.vector.tensor_copy(X(*out), X(*in0)))
+
+    def ms(out, val):
+        return add(G, "v", 64 * CYC, [], [out], lambda: g.vector.memset(X(*out), val))
+
+    def act(out, in0, func, **kw):
+        rd = [in0] + [v for v in kw.values() if isinstance(v, tuple)]
+        return add(G, "a", max(64.0, in0[2] - in0[1]) * CYC + 60, rd, [out],
+                   lambda: g.scalar.activation(X(*out), X(*in0), func, **{nm: Y(v) for nm, v in kw.items()}))
+
+    def gat(q, out, win, off):
+        def fn():
+            w = X(*win).indirect(X(*off))
+            return g.vector.tensor_copy(X(*out), w) if q == "v" else g.scalar.activation(X(*out), w, F.Copy)
+        return add(G, q, 60 + (out[2] - out[1]) * GF * CYC, [win, off], [out], fn)
+
+    def gtt(out, win, off, in1, op):
+        return add(G, "v", 60 + (out[2] - out[1]) * GF * CYC, [win, off, in1], [out],
+                   lambda: g.vector.tensor_tensor(X(*out), X(*win).indirect(X(*off)), X(*in1), op))
+
+    def mm(outs, lhs, rhs, start, stop):
+        return add(G, "p", max(64, rhs[2] - rhs[1]) * 0.6, [lhs, rhs], [outs],
+                   lambda: g.tensor.matmul(X(*outs), X(*lhs), X(*rhs), start, stop))
+
+    def ext(ps, zname, src, v0, v1):
+        w = (v1 - v0) // 16
+
+        def fn():
+            for i in range(16):
+                ins = g.tensor.matmul(T[ps][:, 0:w], T[zname][:, 15 - i:143 - i], T[src][:, v0 + i:v1:16], i == 0, i == 15)
+            return ins
+        return add(G, "p", 16 * max(64, w) * 0.6, [(zname, 0, 144), (src, v0, v1)], [(ps, 0, 512)], fn)
+
+    def spread(ps, c0):
+        def fn():
+            for i in range(16):
+                o = T[ps][:, i:512:16]
+                g.tensor.matmul(o, T["yb"][:, 16 + 128 * i:144 + 128 * i], T["hib"][:, c0:c0 + 32], True, False)
+                ins = g.tensor.matmul(o, T["yb"][:, 15 + 128 * i:143 + 128 * i], T["lob"][:, c0:c0 + 32], False, True)
+            return ins
+        return add(G, "p", 32 * 64 * 0.6, [("yb", 0, 2064), ("hib", c0, c0 + 32), ("lob", c0, c0 + 32)], [(ps, 0, 512)], fn)
+
+    nst = [0]
+
+    def load(q, k, out, src, lat=2000.0):
+        eng = g.sync if q == "s" else g.scalar
+        return add(G, q, lat, [], [out], lambda: eng.dma_start(X(*out), src), "d", "ld%d" % k, 16)
+
+    def store(dst, src):
+        k = nst[0]
+        nst[0] += 1
+        return add(G, "s", 2000.0, [src], [], lambda: g.sync.dma_start(dst, X(*src)), "d", "st%d" % k, 16)
+
+    peers = [c for c in T.cores if c != core]
+    near = [c for c in peers if topo.chip(c) == topo.chip(core)]
+    far = [c for c in peers if topo.chip(c) != topo.chip(core)]
+    efar = [e for e in topo.engines(core, far[0]) if all(e in topo.engines(core, c) for c in far)]
+    enear = [e for e in topo.engines(core, near[0]) if e not in efar]
+    nloc = [0]
+
+    def share(buf, sem, lat):
+        c0 = r * B
+
+        def fn():
+            tr = []
+            for dsts, eng in ((far, efar), (near, enear)):
+                ids = []
+                for c in dsts:
+                    rid, pid, se = topo.addr(c)
+                    ids.append(DstId(rid=rid, pnc=pid))
+                tr.append(RemoteDMATransfer(dst_ids=ids, dma_engine_mask=sum(1 << e for e in eng), remote_sem=T.sem[sem],
+                                            srcs=[X(buf, c0, c0 + B)], dsts=[X(buf, c0, c0 + B)] * len(ids)))
+            return g.remote_dma_fused(tr, local_sem=T.sem.ls)
+        nloc[0] += len(efar) + len(enear)
+        i = add(G, "g", 1000.0, [(buf, c0, c0 + B)], [], fn, "s")
+        tot = 0
+        for c in peers:
+            f2 = [x for x in T.cores if topo.chip(x) != topo.chip(c)]
+            e2 = topo.engines(c, f2[0])
+            tot += len(e2) if topo.chip(c) != topo.chip(core) else len([e for e in topo.engines(c, core) if e not in e2])
+        wr = [(buf, a, b) for (a, b) in ((0, c0), (c0 + B, M)) if b > a]
+        add(G, "n", lat, [], wr, None, "n", sem, tot, deps=[i])
+
+    def own(v0, v1):
+        o = r * B if v1 <= B else M - B
+        return (v0 + o, v1 + o)
+
+    load("s", 0, ("parI", 0, 32), T.par[:, 0:32])
+    load("a", 1, ("qraw", 0, B), T.q[:, 0:B])
+    load("s", 2, ("parI", 32, 128), T.par[:, 32:128])
+    load("s", 3, ("am", 0, 128), T.amat[:, :])
+    load("s", 4, ("thI", 0, 1), T.th[:, :])
+    load("s", 5, ("qraw", B, V), T.q[:, B:V], 3000.0)
+    load("s", 6, ("clrs", 0, 4096), T.clr[:, :], 5000.0)
+
+    def io(out, pattern, base, cm, flag):
+        kw = {"allow_small_or_imprecise_dtypes": True} if flag else {}
+        return add(G, "g", 130 + 2 * (out[2] - out[1]) * CYC, [], [out], lambda: g.iota(X(*out), pattern, base, cm, **kw))
+    io(("pI", 0, 1), [[0, 1]], 0, 1, False)
+    io(("rowg", 0, 8), [[16, 8]], 0, 0, True)
+    io(("row", 0, 16), [[1, 16]], 0, 0, True)
+    io(("own0", 0, 32), [[16, 32]], r * B, 0, True)
+    io(("own0", 32, 128), [[16, 96]], M, 0, True)
+    ts(("pmI", 0, 1), ("pI", 0, 1), 15, A.bitwise_and)
+    tc(("pm", 0, 1), ("pmI", 0, 1))
+    tt(("pd", 0, 1), ("pI", 0, 1), ("pm", 0, 1), A.subtract)
+    ts(("oh", 0, 16), ("row", 0, 16), ("pm", 0, 1), A.is_equal)
+    ms(("z", 0, 144), 0.0)
+    ts(("z", 15, 128, 16), ("rowg", 0, 8), ("pd", 0, 1), A.is_equal)
+    ms(("yb", 0, 16), 0.0)
+    for i in range(16):
+        ts(("yb", 16 + 128 * i, 144 + 128 * i), ("z", 15, 143), ("oh", i, i + 1), A.mult, fast=True)
+
+    def names0(c0, c1):
+        ts(("hiI", c0, c1), ("parI", c0, c1), 4, A.arith_shift_right)
+        ts(("loI", c0, c1), ("parI", c0, c1), 15, A.bitwise_and)
+        tc(("hib", c0, c1), ("hiI", c0, c1))
+        tc(("lob", c0, c1), ("loI", c0, c1))
+        for b in range(c0, c1, 32):
+            ps = "ps%d" % (3 + (b // 32))
+            spread(ps, b)
+            a0, a1 = own(16 * b, 16 * b + 512)
+            if b == 0:
+                tc(("nw0", a0, a1), (ps, 0, 512))
+            else:
+                act(("nw0", a0, a1), (ps, 0, 512), F.Copy)
+    names0(0, 32)
+    share("nw0", "an0", 3000.0)
+    a0, a1 = own(0, B)
+    ts(("Q0", a0, a1), ("qraw", 0, B), 128.0, A.add, fast=True)
+    share("Q0", "aq0", 3000.0)
+    ts(("wn", 0, 1), ("oh", 0, 1), 16.0, A.mult, ("oh", 1, 2), A.add)
+    ms(("pw", 12, 16), 0.0)
+    for i in range(12):
+        ms(("pw", i, i + 1), float(2 ** i))
+    tt(("pwo", 0, 16), ("pw", 0, 16), ("oh", 0, 16), A.mult)
+    for h in (8, 4, 2, 1):
+        tt(("pwo", 0, h), ("pwo", 0, h), ("pwo", h, 2 * h), A.add)
+    ts(("zn", 0, 144), ("z", 0, 144), ("wn", 0, 1), A.mult, fast=True)
+    ts(("zc", 0, 144), ("z", 0, 144), ("pwo", 0, 1), A.mult, fast=True)
+    ts(("own", 0, 128), ("own0", 0, 128), ("pm", 0, 1), A.add)
+    for (c0, c1) in ((0, 32), (32, 128)):
+        tc(("nf0", c0, c1), ("parI", c0, c1))
+        tc(("n16_0", c0, c1), ("parI", c0, c1))
+        tt(("dn0", c0, c1), ("nf0", c0, c1), ("own", c0, c1), A.subtract)
+    ms(("ones", 0, 16), 1.0)
+    mm(("ps7", 0, 2), ("am", 0, 128), ("ones", 0, 2), True, True)
+    tc(("thf", 0, 1), ("thI", 0, 1))
+    ts(("thr", 0, 1), ("ps7", 0, 1), 256.5, A.mult, ("thf", 0, 1), A.add)
+    for k in range(RO):
+        ts(("bias", k, k + 1), ("thr", 0, 1), 0.5, A.add, -float(2 ** k), A.mult)
+    ts(("am2", 0, 128), ("am", 0, 128), 2.0, A.mult, fast=True)
+    names0(32, 128)
+    a0, a1 = own(B, V)
+    ts(("Q0", a0, a1), ("qraw", B, V), 128.0, A.add, fast=True)
+
+    sb = [0]
+    for k in range(RO):
+        P = k % 2
+        Qk, Qn, Nk = "Q%d" % k, "Q%d" % (k + 1), "nw%d" % k
+        for ci, (v0, v1, sub) in enumerate(CH):
+            w0, w1 = v0 // 16, v1 // 16
+            we = M if ci == 0 else W
+            subs = [(x, x + sub) for x in range(v0, v1, sub)]
+            eps = "ps%d" % ci
+            L = lambda nm: ("%s%d" % (nm, P), w0, w1)
+            nf = ("nf%d" % k, w0, w1)
+            for x, y in subs:
+                gat("a" if ci or x == v0 else "v", ("hb%d" % P, x, y), (Nk, 0, we), ("n16_%d" % k, x // 16, y // 16))
+            ext(eps, "zn", "hb%d" % P, v0, v1)
+            tc(L("h16_"), (eps, 0, w1 - w0))
+            tt(L("dh"), (eps, 0, w1 - w0), nf, A.subtract)
+            for x, y in subs:
+                a0, a1 = own(x, y)
+                ts(("ah%d" % P, x, y), (Qk, a0, a1), -0.5 * 2 ** k, A.add, fast=True)
+                if ci == 0:
+                    ps = "ps%d" % (3 + (x - v0) // sub)
+                else:
+                    ps = "ps%d" % (5 + sb[0] % 3)
+                    sb[0] += 1
+                mm((ps, 0, y - x), ("am2", 0, 128), (Qk, a0, a1), True, False)
+                gtt(("e%d" % P, x, y), (Qk, 0, we), ("h16_%d" % P, x // 16, y // 16), ("ah%d" % P, x, y), A.subtract)
+                mm((ps, 0, y - x), ("am", 0, 128), ("e%d" % P, x, y), False, True)
+                act(("bits%d" % P, x, y), (ps, 0, y - x), F.Sign, bias=("bias", k, k + 1))
+            ext(eps, "zc", "bits%d" % P, v0, v1)
+            ts(L("c16_"), (eps, 0, w1 - w0), 0.5, A.mult, 2047.5, A.add)
+            for x, y in subs:
+                act(("ae%d" % P, x, y), ("e%d" % P, x, y), F.Abs, scale=float(2.0 ** -k), bias=-0.5)
+            for x, y in subs:
+                gtt(("okb%d" % P, x, y), ("clrs", 0, 4096), ("c16_%d" % P, x // 16, y // 16), ("ae%d" % P, x, y), A.is_ge)
+            ext(eps, "z", "okb%d" % P, v0, v1)
+            ts(L("okm"), (eps, 0, w1 - w0), 15.5, A.is_ge)
+            tt(L("t"), L("okm"), L("dn"), A.mult)
+            l3, l4 = ("l34_%d" % P, 2 * w0, w0 + w1), ("l34_%d" % P, w0 + w1, 2 * w1)
+            tt(l3, nf, L("t"), A.subtract)
+            if k < RO - 1:
+                tt(l4, ("own", w0, w1), L("t"), A.add)
+                tc(("l16_%d" % P, 2 * w0, 2 * w1), ("l34_%d" % P, 2 * w0, 2 * w1))
+                for x, y in subs:
+                    a0, a1 = own(x, y)
+                    o = w0 + w1 + (x - v0) // 16
+                    gat("a", ("nw%d" % (k + 1), a0, a1), (Nk, 0, we), ("l16_%d" % P, o, o + (y - x) // 16))
+                if ci == 0:
+                    share("nw%d" % (k + 1), "an%d" % (k + 1), 3000.0)
+            else:
+                tc(("l16_%d" % P, 2 * w0, w0 + w1), l3)
+            for x, y in subs:
+                a0, a1 = own(x, y)
+                o = 2 * w0 + (x - v0) // 16
+                gtt((Qn, a0, a1), (Qk, 0, we), ("l16_%d" % P, o, o + (y - x) // 16), ("ah%d" % P, x, y), A.add)
+                if k == RO - 1:
+                    if y < v1:
+                        act(("yout", x, y), (Qn, a0, a1), F.Identity, scale=float(2.0 ** -RO), bias=-128.0)
+                    else:
+                        ts(("yout", x, y), (Qn, a0, a1), 2.0 ** -RO, A.mult, -128.0, A.add, fast=True)
+            if k == RO - 1:
+                store(T.yq[:, v0:v1], ("yout", v0, v1))
+            elif ci == 0:
+                share(Qn, "aq%d" % (k + 1), 3000.0)
+            tt(L("t2"), L("okm"), L("dh"), A.mult)
+            tt(("nf%d" % (k + 1), w0, w1), nf, L("t2"), A.add)
+            if k < RO - 1:
+                tc(("n16_%d" % (k + 1), w0, w1), ("nf%d" % (k + 1), w0, w1))
+                tt(("dn%d" % (1 - P), w0, w1), ("nf%d" % (k + 1), w0, w1), ("own", w0, w1), A.subtract)
+            else:
+                store(T.yp[:, w0:w1], ("nf%d" % RO, w0, w1))
+    return G, nloc[0]
+
+
+def rank_program(g, core, T, topo):
+    if T.rank_of(core) is None:
+        return
+    G, nloc = build(g, core, T, topo)
+    ops = G["ops"]
+    start, fin = schedule(ops)
+    eng = {"v": g.vector, "a": g.scalar, "p": g.tensor, "g": g, "s": g.sync}
+    cnt = {"v": 0, "a": 0, "p": 0, "g": 0}
+    known = {q: {} for q in eng}
+    tok, snap = {}, {}
+
+    def wait(q, d):
+        s, v = tok[d]
+        k = known[q]
+        if k.get(s, 0) >= v:
+            return
+        eng[q].wait_ge(T.sem[s], v)
+        for a, b in snap[d].items():
+            if k.get(a, 0) < b:
+                k[a] = b
+    for i in sorted(range(len(ops)), key=lambda i: (start[i], i)):
+        o = ops[i]
+        q = o["q"]
+        if o["kind"] == "n":
+            tok[i] = (o["sem"], o["val"])
+            snap[i] = {o["sem"]: o["val"]}
+            continue
+        for d in sorted(o["edges"], key=lambda d: -fin[d]):
+            if q == "p" and ops[d]["q"] == "p" and not o["edges"][d]:
+                continue
+            if ops[d]["kind"] != "s":
+                wait(q, d)
+        ins = o["fn"]()
+        if o["kind"] == "c":
+            cnt[q] += 1
+            tok[i] = (QSEM[q], cnt[q])
+            ins.then_inc(T.sem[QSEM[q]], 1)
+        elif o["kind"] == "d":
+            tok[i] = (o["sem"], o["val"])
+            ins.then_inc(T.sem[o["sem"]], 16)
+        if o["kind"] != "s":
+            snap[i] = dict(known[q])
+            snap[i][tok[i][0]] = tok[i][1]
+    g.wait_ge(T.sem.ls, nloc)
+    for i in range(len(ops)):
+        if ops[i]["kind"] in ("d", "n"):
+            wait("s", i)
+    for q in cnt:
+        if known["s"].get(QSEM[q], 0) < cnt[q]:
+            g.sync.wait_ge(T.sem[QSEM[q]], cnt[q])

@@ -4,57 +4,78 @@ from concourse.mybir import AluOpType, ActivationFunctionType
 N, V, B, RO = 4, 2048, 512, 5
 M = N * B
 W = M + V - B
-CH = [(0, 512, 256), (512, 1280, 384), (1280, 2048, 384)]
+
+CHUNKS = [
+    {"c": (0, 512), "hb": "a256 v256", "e": "v256 a256", "ah": "a512", "ok": "v512", "nw": "a256 v256", "up": "v512"},
+    {"c": (512, 1280), "hb": "a768", "e": "v768", "ah": "v768", "ok": "v768", "nw": "a768", "up": "v768"},
+    {"c": (1280, 2048), "hb": "a256 a256 v256", "e": "a384 v384", "ah": "v768", "ok": "v768", "nw": "a384 a384", "up": "v384 v384"},
+]
+EPS = ["ps0", "ps1", "ps2"]
+SUMS = ["ps3", "ps4", "ps5", "ps6", "ps7"]
 
 SCRATCH = {}
-_BF, _F32, _I32, _U16 = "bfloat16", "float32", "int32", "uint16"
+_BF, _FH, _F32, _I32, _U16 = "bfloat16", "float16", "float32", "int32", "uint16"
 for _nm, _n, _d in (
-        [(x, 128, _I32) for x in ("parI", "hiI", "loI")] + [(x, 128, _BF) for x in ("hib", "lob", "am", "am2")]
+        [(x, 128, _I32) for x in ("parI", "hiI", "loI", "lw")] + [(x, 128, _BF) for x in ("hib", "lob", "am", "am2", "idp", "idn")]
         + [(x, V, _BF) for x in ("qraw", "yout")] + [("clrs", 4096, _BF), ("ones", 16, _BF), ("yb", 16 + 2048, _BF)]
-        + [(x, 144, _BF) for x in ("z", "zn", "zc")] + [(x, 1, _I32) for x in ("thI", "pI", "pmI")]
-        + [(x, 1, _F32) for x in ("thf", "thr", "pm", "pd", "wn")] + [("bias", 8, _F32), ("rowg", 8, _F32)]
-        + [(x, 16, _F32) for x in ("row", "oh", "pw", "pwo")] + [(x, 128, _F32) for x in ("own0", "own")]
+        + [(x, 144, _BF) for x in ("z", "zn", "zc")] + [("zh", 144, _FH)] + [(x, 1, _I32) for x in ("thI", "pI", "pmI")]
+        + [(x, 1, _F32) for x in ("thf", "thr", "thd", "pm", "pd", "wn")] + [(x, 8, _F32) for x in ("bias", "biasd", "rowg")]
+        + [(x, 16, _F32) for x in ("row", "oh", "pw", "pwo")] + [(x, 128, _F32) for x in ("own0", "own", "rowp")]
+        + [("hbh", B, _FH), ("mask", B, _BF), ("lo16", 32, _U16), ("hi16", 32, _U16)]
         + [("Q%d" % k, W, _BF) for k in range(RO + 1)] + [("nf%d" % k, 128, _F32) for k in range(RO + 1)]
         + [("nw%d" % k, W, _BF) for k in range(RO)] + [("n16_%d" % k, 128, _U16) for k in range(RO)]
         + [("%s%d" % (x, k), V, _BF) for k in range(2) for x in ("hb", "bits", "okb", "e", "ae")]
-        + [("ah%d" % k, V, "float16") for k in range(2)]
-        + [("%s%d" % (x, k), 128, _F32) for k in range(2) for x in ("dn", "dh", "okm", "t", "t2")]
+        + [("ah%d" % k, V, _FH) for k in range(2)] + [("af%d" % k, V, _F32) for k in range(2)]
+        + [("%s%d" % (x, k), 128, _F32) for k in range(2) for x in ("dn", "dh")]
         + [("%s%d" % (x, k), 128, _U16) for k in range(2) for x in ("h16_", "c16_")]
         + [("l34_%d" % k, 256, _F32) for k in range(2)] + [("l16_%d" % k, 256, _U16) for k in range(2)]):
     SCRATCH[_nm] = ("sbuf", [128, _n], _d)
 for _k in range(8):
     SCRATCH["ps%d" % _k] = ("psum", [128, 512], "float32")
-SEMAPHORES = ["sv", "sa", "sp", "sg", "ls"] + ["%s%d" % (x, k) for x in ("an", "aq") for k in range(RO)] \
-    + ["%s%d" % (x, k) for x in ("ld", "st") for k in range(8)]
-
-CYC, WAKE, GF = 0.83, 90.0, 1.56
+SEMAPHORES = ["sv", "sa", "sp", "sg", "ls", "al"] + ["%s%d" % (x, k) for x in ("an", "aq") for k in range(RO)] \
+    + ["%s%d" % (x, k) for x in ("ld", "st") for k in range(12)]
 QSEM = {"v": "sv", "a": "sa", "p": "sp", "g": "sg"}
 
+FAC, GEL, PE, WAKE, SAME, ISSUE, FLIGHT, DMA = 1.15, 1.56, 0.5, 90.0, 30.0, 700.0, 3000.0, 2000.0
+LEAD = {"0 gat hb": -20249, "i ts Q": -9028, "k0 c0": -2637, "0 act yout": -2259, "k0 c2": -3217, "0 tt dh": 24050, "0 act ae": -1574,
+        "2 gat hb": 1436, "0 gtt Q": -2179, "2 tc n16_": -5807, "i ms pw": -18957, "i ts thr": -4266, "0 tc h16_": 2660,
+        "1 tt l34_": 8487, "1 ts ah": -17644, "1 tc l16_": 10989, "k4 c2": -7641, "1 gat hb": -7582, "2 gtt Q": -1943, "k4 c0": -1459}
 
-def add(G, q, cost, reads, writes, fn, kind="c", sem=None, val=0, deps=()):
+
+def cost(kind, q, c):
+    if kind == "d":
+        return DMA + c[0]
+    if kind == "s":
+        return ISSUE
+    if kind == "n":
+        return FLIGHT
+    return FAC * (PE * c[1] if q == "p" else c[0] + 0.83 * (c[1] + GEL * c[2]))
+
+
+def add(G, q, c, reads, writes, fn, kind="c", sem=None, val=0, deps=(), tag=""):
     i = len(G["ops"])
     edges = {d: True for d in deps}
     for kindrw, regs in ((0, reads), (1, writes)):
         for (nm, c0, c1) in regs:
             psum = nm[:2] == "ps"
-            if psum:
-                c0, c1 = 0, 512
             for (a0, a1, o, w) in G["hist"].setdefault(nm, []):
-                if o == i or a0 >= c1 or c0 >= a1:
+                other = psum and G["ops"][o]["q"] != q
+                if not other and (a0 >= c1 or c0 >= a1):
                     continue
                 if w and not kindrw:
                     edges[o] = True
-                elif kindrw or (psum and G["ops"][o]["q"] != q):
+                elif kindrw or other:
                     edges.setdefault(o, False)
     for kindrw, regs in ((0, reads), (1, writes)):
         for (nm, c0, c1) in regs:
-            if nm[:2] == "ps":
-                c0, c1 = 0, 512
             h = G["hist"][nm]
+            psum = nm[:2] == "ps"
             if kindrw:
-                h[:] = [x for x in h if not (x[0] >= c0 and x[1] <= c1)]
+                h[:] = [x for x in h if not ((psum and q == "p") or (x[0] >= c0 and x[1] <= c1 and (
+                    not psum or x[2] == i or G["ops"][x[2]]["q"] == q)))]
             h.append((c0, c1, i, kindrw))
-    G["ops"].append({"q": q, "cost": cost, "fn": fn, "kind": kind, "sem": sem, "val": val, "edges": edges})
+    lead = LEAD.get("%s %s" % (G["c"], tag), 0.0) + LEAD.get("k%d c%s" % (G["k"], G["c"]), 0.0)
+    G["ops"].append({"q": q, "cost": cost(kind, q, c), "fn": fn, "kind": kind, "sem": sem, "val": val, "edges": edges, "lead": lead})
     return i
 
 
@@ -64,46 +85,47 @@ def schedule(ops):
     for i, o in enumerate(ops):
         for d in o["edges"]:
             succ[d].append(i)
-    pri = [0.0] * n
+    step = lambda a, b: WAKE if ops[a]["q"] != ops[b]["q"] else SAME
+    way = [0.0] * n
     for i in range(n - 1, -1, -1):
-        pri[i] = ops[i]["cost"] + max([pri[s] + (WAKE if ops[s]["q"] != ops[i]["q"] else 20.0) for s in succ[i]] or [0.0])
+        way[i] = ops[i]["cost"] + max([way[s] + step(i, s) for s in succ[i]] or [0.0])
+    pri = [w + o["lead"] for w, o in zip(way, ops)]
     left = [len(o["edges"]) for o in ops]
     ready, free = {}, {}
-    rt, start, fin = [0.0] * n, [0.0] * n, [0.0] * n
+    rt, start = [0.0] * n, [0.0] * n
     for i in range(n):
         if left[i] == 0:
             ready.setdefault(ops[i]["q"], []).append(i)
     for _ in range(n):
         best = None
-        for q, lst in ready.items():
+        for q in sorted(ready):
+            lst = ready[q]
             if not lst:
                 continue
-            if q == "n":
-                c = min(lst, key=lambda i: rt[i])
-                s = rt[c]
-            else:
-                s = max(free.get(q, 0.0), min(rt[i] for i in lst))
-                c = max((i for i in lst if rt[i] <= s + 1e-9), key=lambda i: pri[i])
+            first = min(rt[i] for i in lst)
+            s = first if q == "n" else max(free.get(q, 0.0), first)
             if best is None or s < best[0]:
-                best = (s, q, c)
+                best = (s, q, max((i for i in lst if rt[i] <= s + 1e-9), key=lambda i: pri[i]))
         s, q, c = best
         ready[q].remove(c)
-        start[c], fin[c] = s, s + ops[c]["cost"]
-        free[q] = s + (60.0 if ops[c]["kind"] == "d" else ops[c]["cost"])
+        start[c] = s
+        f = s + ops[c]["cost"]
+        free[q] = s + 60.0 if ops[c]["kind"] == "d" else f
         for x in succ[c]:
-            rt[x] = max(rt[x], fin[c] + (WAKE if ops[x]["q"] != q else 20.0))
+            rt[x] = max(rt[x], f + step(c, x))
             left[x] -= 1
             if left[x] == 0:
                 ready.setdefault(ops[x]["q"], []).append(x)
-    return start, fin
+    return sorted(range(n), key=lambda i: (start[i], i))
 
 
 def build(g, core, T, topo):
     A, F = AluOpType, ActivationFunctionType
     r = T.rank_of(core)
-    G = {"ops": [], "hist": {}}
+    G = {"ops": [], "hist": {}, "c": "i", "k": -1}
     X = lambda nm, a, b, s=1: T[nm][:, a:b] if s == 1 else T[nm][:, a:b:s]
     Y = lambda s: X(*s) if isinstance(s, tuple) else s
+    bare = lambda nm: nm.rstrip("0123456789")
 
     def ts(out, in0, s1, op0, s2=None, op1=None, fast=False):
         def fn():
@@ -111,36 +133,40 @@ def build(g, core, T, topo):
                 return g.vector.tensor_scalar(X(*out), X(*in0), Y(s1), None, op0)
             return g.vector.tensor_scalar(X(*out), X(*in0), Y(s1), Y(s2), op0, op1)
         rd = [in0] + [s for s in (s1, s2) if isinstance(s, tuple)]
-        return add(G, "v", max(64.0, (in0[2] - in0[1]) * (0.5 if fast else 1.0)) * CYC, rd, [out[:3]], fn)
+        cyc = max(64.0, (in0[2] - in0[1]) * (0.5 if fast else 1.0))
+        return add(G, "v", (0, cyc, 0), rd, [out[:3]], fn, tag="ts " + bare(out[0]))
 
     def tt(out, in0, in1, op):
-        cost = max(64.0, (in0[2] - in0[1]) * (1.0 if in0[0][:2] == "ps" else 2.0)) * CYC
-        return add(G, "v", cost, [in0, in1], [out], lambda: g.vector.tensor_tensor(X(*out), X(*in0), X(*in1), op))
+        cyc = max(64.0, (in0[2] - in0[1]) * (1.0 if "ps" in (in0[0][:2], in1[0][:2]) else 2.0))
+        return add(G, "v", (0, cyc, 0), [in0, in1], [out],
+                   lambda: g.vector.tensor_tensor(X(*out), X(*in0), X(*in1), op), tag="tt " + bare(out[0]))
 
     def tc(out, in0):
-        return add(G, "v", max(64.0, in0[2] - in0[1]) * CYC, [in0], [out], lambda: g.vector.tensor_copy(X(*out), X(*in0)))
+        return add(G, "v", (0, max(64.0, in0[2] - in0[1]), 0), [in0], [out],
+                   lambda: g.vector.tensor_copy(X(*out), X(*in0)), tag="tc " + bare(out[0]))
 
     def ms(out, val):
-        return add(G, "v", 64 * CYC, [], [out], lambda: g.vector.memset(X(*out), val))
+        return add(G, "v", (0, 64, 0), [], [out], lambda: g.vector.memset(X(*out), val), tag="ms " + bare(out[0]))
 
     def act(out, in0, func, **kw):
         rd = [in0] + [v for v in kw.values() if isinstance(v, tuple)]
-        return add(G, "a", max(64.0, in0[2] - in0[1]) * CYC + 60, rd, [out],
-                   lambda: g.scalar.activation(X(*out), X(*in0), func, **{nm: Y(v) for nm, v in kw.items()}))
+        return add(G, "a", (40, max(64.0, in0[2] - in0[1]), 0), rd, [out],
+                   lambda: g.scalar.activation(X(*out), X(*in0), func, **{nm: Y(v) for nm, v in kw.items()}),
+                   tag="act " + bare(out[0]))
 
     def gat(q, out, win, off):
         def fn():
             w = X(*win).indirect(X(*off))
             return g.vector.tensor_copy(X(*out), w) if q == "v" else g.scalar.activation(X(*out), w, F.Copy)
-        return add(G, q, 60 + (out[2] - out[1]) * GF * CYC, [win, off], [out], fn)
+        return add(G, q, (50 if q == "v" else 65, 0, out[2] - out[1]), [win, off], [out], fn, tag="gat " + bare(out[0]))
 
     def gtt(out, win, off, in1, op):
-        return add(G, "v", 60 + (out[2] - out[1]) * GF * CYC, [win, off, in1], [out],
-                   lambda: g.vector.tensor_tensor(X(*out), X(*win).indirect(X(*off)), X(*in1), op))
+        return add(G, "v", (50, 0, out[2] - out[1]), [win, off, in1], [out],
+                   lambda: g.vector.tensor_tensor(X(*out), X(*win).indirect(X(*off)), X(*in1), op), tag="gtt " + bare(out[0]))
 
     def mm(outs, lhs, rhs, start, stop):
-        return add(G, "p", max(64, rhs[2] - rhs[1]) * 0.6, [lhs, rhs], [outs],
-                   lambda: g.tensor.matmul(X(*outs), X(*lhs), X(*rhs), start, stop))
+        return add(G, "p", (0, max(64, rhs[2] - rhs[1]), 0), [lhs, rhs], [outs],
+                   lambda: g.tensor.matmul(X(*outs), X(*lhs), X(*rhs), start, stop), tag="mm")
 
     def ext(ps, zname, src, v0, v1):
         w = (v1 - v0) // 16
@@ -149,7 +175,7 @@ def build(g, core, T, topo):
             for i in range(16):
                 ins = g.tensor.matmul(T[ps][:, 0:w], T[zname][:, 15 - i:143 - i], T[src][:, v0 + i:v1:16], i == 0, i == 15)
             return ins
-        return add(G, "p", 16 * max(64, w) * 0.6, [(zname, 0, 144), (src, v0, v1)], [(ps, 0, 512)], fn)
+        return add(G, "p", (0, 16 * max(64, w), 0), [(zname, 0, 144), (src, v0, v1)], [(ps, 0, w)], fn, tag="ext " + bare(src))
 
     def spread(ps, c0):
         def fn():
@@ -158,18 +184,19 @@ def build(g, core, T, topo):
                 g.tensor.matmul(o, T["yb"][:, 16 + 128 * i:144 + 128 * i], T["hib"][:, c0:c0 + 32], True, False)
                 ins = g.tensor.matmul(o, T["yb"][:, 15 + 128 * i:143 + 128 * i], T["lob"][:, c0:c0 + 32], False, True)
             return ins
-        return add(G, "p", 32 * 64 * 0.6, [("yb", 0, 2064), ("hib", c0, c0 + 32), ("lob", c0, c0 + 32)], [(ps, 0, 512)], fn)
+        return add(G, "p", (0, 32 * 64, 0), [("yb", 0, 2064), ("hib", c0, c0 + 32), ("lob", c0, c0 + 32)], [(ps, 0, 512)], fn,
+                   tag="spread")
 
     nst = [0]
 
-    def load(q, k, out, src, lat=2000.0):
+    def load(q, k, out, src, more=0.0):
         eng = g.sync if q == "s" else g.scalar
-        return add(G, q, lat, [], [out], lambda: eng.dma_start(X(*out), src), "d", "ld%d" % k, 16)
+        return add(G, q, (more,), [], [out], lambda: eng.dma_start(X(*out), src), "d", "ld%d" % k, 16, tag="load")
 
     def store(dst, src):
         k = nst[0]
         nst[0] += 1
-        return add(G, "s", 2000.0, [src], [], lambda: g.sync.dma_start(dst, X(*src)), "d", "st%d" % k, 16)
+        return add(G, "s", (0.0,), [src], [], lambda: g.sync.dma_start(dst, X(*src)), "d", "st%d" % k, 16, tag="store")
 
     peers = [c for c in T.cores if c != core]
     near = [c for c in peers if topo.chip(c) == topo.chip(core)]
@@ -178,8 +205,8 @@ def build(g, core, T, topo):
     enear = [e for e in topo.engines(core, near[0]) if e not in efar]
     nloc = [0]
 
-    def share(buf, sem, lat):
-        c0 = r * B
+    def share(buf, sem, cols, step):
+        c0, c1 = cols
 
         def fn():
             tr = []
@@ -189,66 +216,77 @@ def build(g, core, T, topo):
                     rid, pid, se = topo.addr(c)
                     ids.append(DstId(rid=rid, pnc=pid))
                 tr.append(RemoteDMATransfer(dst_ids=ids, dma_engine_mask=sum(1 << e for e in eng), remote_sem=T.sem[sem],
-                                            srcs=[X(buf, c0, c0 + B)], dsts=[X(buf, c0, c0 + B)] * len(ids)))
+                                            srcs=[X(buf, c0, c1)], dsts=[X(buf, c0, c1)] * len(ids)))
             return g.remote_dma_fused(tr, local_sem=T.sem.ls)
         nloc[0] += len(efar) + len(enear)
-        i = add(G, "g", 1000.0, [(buf, c0, c0 + B)], [], fn, "s")
+        i = add(G, "g", (0.0,), [(buf, c0, c1)], [], fn, "s", tag="share " + bare(buf))
         tot = 0
         for c in peers:
             f2 = [x for x in T.cores if topo.chip(x) != topo.chip(c)]
             e2 = topo.engines(c, f2[0])
             tot += len(e2) if topo.chip(c) != topo.chip(core) else len([e for e in topo.engines(c, core) if e not in e2])
-        wr = [(buf, a, b) for (a, b) in ((0, c0), (c0 + B, M)) if b > a]
-        add(G, "n", lat, [], wr, None, "n", sem, tot, deps=[i])
+        wr = [(buf, a, b) for (a, b) in ((0, c0), (c1, N * step)) if b > a]
+        add(G, "n", (0.0,), [], wr, None, "n", sem, tot, deps=[i], tag="arr " + bare(buf))
 
     def own(v0, v1):
         o = r * B if v1 <= B else M - B
         return (v0 + o, v1 + o)
 
-    load("s", 0, ("parI", 0, 32), T.par[:, 0:32])
+    mine = ("lw", 32 * r, 32 * r + 32)
+    load("s", 0, mine, T.par[:, 0:32])
     load("a", 1, ("qraw", 0, B), T.q[:, 0:B])
     load("s", 2, ("parI", 32, 128), T.par[:, 32:128])
     load("s", 3, ("am", 0, 128), T.amat[:, :])
     load("s", 4, ("thI", 0, 1), T.th[:, :])
-    load("s", 5, ("qraw", B, V), T.q[:, B:V], 3000.0)
-    load("s", 6, ("clrs", 0, 4096), T.clr[:, :], 5000.0)
+    load("s", 5, ("qraw", B, V), T.q[:, B:V], 1000.0)
+    load("s", 6, ("clrs", 0, 4096), T.clr[:, :], 3000.0)
 
     def io(out, pattern, base, cm, flag):
         kw = {"allow_small_or_imprecise_dtypes": True} if flag else {}
-        return add(G, "g", 130 + 2 * (out[2] - out[1]) * CYC, [], [out], lambda: g.iota(X(*out), pattern, base, cm, **kw))
+        return add(G, "g", (130, 2 * (out[2] - out[1]), 0), [], [out], lambda: g.iota(X(*out), pattern, base, cm, **kw), tag="iota")
     io(("pI", 0, 1), [[0, 1]], 0, 1, False)
     io(("rowg", 0, 8), [[16, 8]], 0, 0, True)
     io(("row", 0, 16), [[1, 16]], 0, 0, True)
     io(("own0", 0, 32), [[16, 32]], r * B, 0, True)
     io(("own0", 32, 128), [[16, 96]], M, 0, True)
+    io(("rowp", 0, 128), [[1, 128]], 0, -1, True)
     ts(("pmI", 0, 1), ("pI", 0, 1), 15, A.bitwise_and)
     tc(("pm", 0, 1), ("pmI", 0, 1))
     tt(("pd", 0, 1), ("pI", 0, 1), ("pm", 0, 1), A.subtract)
     ts(("oh", 0, 16), ("row", 0, 16), ("pm", 0, 1), A.is_equal)
     ms(("z", 0, 144), 0.0)
     ts(("z", 15, 128, 16), ("rowg", 0, 8), ("pd", 0, 1), A.is_equal)
+    tc(("zh", 0, 144), ("z", 0, 144))
     ms(("yb", 0, 16), 0.0)
     for i in range(16):
         ts(("yb", 16 + 128 * i, 144 + 128 * i), ("z", 15, 143), ("oh", i, i + 1), A.mult, fast=True)
 
     def names0(c0, c1):
-        ts(("hiI", c0, c1), ("parI", c0, c1), 4, A.arith_shift_right)
-        ts(("loI", c0, c1), ("parI", c0, c1), 15, A.bitwise_and)
+        src = mine if c0 == 0 else ("parI", c0, c1)
+        ts(("hiI", c0, c1), src, 4, A.arith_shift_right)
+        ts(("loI", c0, c1), src, 15, A.bitwise_and)
         tc(("hib", c0, c1), ("hiI", c0, c1))
         tc(("lob", c0, c1), ("loI", c0, c1))
+        if c0 == 0:
+            tc(("lo16", 0, 32), ("loI", 0, 32))
+            tc(("hi16", 0, 32), ("hiI", 0, 32))
+            for x in (0, 256):
+                gat("a" if x else "v", ("mask", x, x + 256), ("oh", 0, 16), ("lo16", x // 16, x // 16 + 16))
         for b in range(c0, c1, 32):
             ps = "ps%d" % (3 + (b // 32))
             spread(ps, b)
             a0, a1 = own(16 * b, 16 * b + 512)
+            act(("nw0", a0, a0 + 256), (ps, 0, 256), F.Copy)
             if b == 0:
-                tc(("nw0", a0, a1), (ps, 0, 512))
+                tc(("nw0", a0 + 256, a1), (ps, 256, 512))
             else:
-                act(("nw0", a0, a1), (ps, 0, 512), F.Copy)
-    names0(0, 32)
-    share("nw0", "an0", 3000.0)
+                act(("nw0", a0 + 256, a1), (ps, 256, 512), F.Copy)
+    share("lw", "al", mine[1:], 32)
     a0, a1 = own(0, B)
     ts(("Q0", a0, a1), ("qraw", 0, B), 128.0, A.add, fast=True)
-    share("Q0", "aq0", 3000.0)
+    share("Q0", "aq0", own(0, B), B)
+    names0(0, 32)
+    share("nw0", "an0", own(0, B), B)
     ts(("wn", 0, 1), ("oh", 0, 1), 16.0, A.mult, ("oh", 1, 2), A.add)
     ms(("pw", 12, 16), 0.0)
     for i in range(12):
@@ -259,89 +297,128 @@ def build(g, core, T, topo):
     ts(("zn", 0, 144), ("z", 0, 144), ("wn", 0, 1), A.mult, fast=True)
     ts(("zc", 0, 144), ("z", 0, 144), ("pwo", 0, 1), A.mult, fast=True)
     ts(("own", 0, 128), ("own0", 0, 128), ("pm", 0, 1), A.add)
+    ts(("idp", 0, 128), ("rowp", 0, 128), 0.0, A.is_equal)
+    ts(("idn", 0, 128), ("idp", 0, 128), -1.0, A.mult, fast=True)
     for (c0, c1) in ((0, 32), (32, 128)):
-        tc(("nf0", c0, c1), ("parI", c0, c1))
-        tc(("n16_0", c0, c1), ("parI", c0, c1))
+        src = mine if c0 == 0 else ("parI", c0, c1)
+        tc(("nf0", c0, c1), src)
+        tc(("n16_0", c0, c1), src)
         tt(("dn0", c0, c1), ("nf0", c0, c1), ("own", c0, c1), A.subtract)
     ms(("ones", 0, 16), 1.0)
     mm(("ps7", 0, 2), ("am", 0, 128), ("ones", 0, 2), True, True)
     tc(("thf", 0, 1), ("thI", 0, 1))
     ts(("thr", 0, 1), ("ps7", 0, 1), 256.5, A.mult, ("thf", 0, 1), A.add)
+    ts(("thd", 0, 1), ("ps7", 0, 1), 256.0, A.mult, ("thf", 0, 1), A.add)
     for k in range(RO):
         ts(("bias", k, k + 1), ("thr", 0, 1), 0.5, A.add, -float(2 ** k), A.mult)
+        ts(("biasd", k, k + 1), ("thd", 0, 1), 0.5, A.add, -float(2 ** k), A.mult)
     ts(("am2", 0, 128), ("am", 0, 128), 2.0, A.mult, fast=True)
     names0(32, 128)
     a0, a1 = own(B, V)
     ts(("Q0", a0, a1), ("qraw", B, V), 128.0, A.add, fast=True)
 
     sb = [0]
+
+    def bank():
+        sb[0] += 1
+        return SUMS[(sb[0] - 1) % len(SUMS)]
+
+    def cut(text, x):
+        out = []
+        for t in text.split():
+            out.append((x, x + int(t[1:]), t[0]))
+            x = out[-1][1]
+        return out
+
+    def halves(x, y):
+        m = -(-(y - x) // 512)
+        return [(x + (y - x) * j // m, x + (y - x) * (j + 1) // m) for j in range(m)]
+
     for k in range(RO):
         P = k % 2
-        Qk, Qn, Nk = "Q%d" % k, "Q%d" % (k + 1), "nw%d" % k
-        for ci, (v0, v1, sub) in enumerate(CH):
+        Qk, Qn, Nk, e = "Q%d" % k, "Q%d" % (k + 1), "nw%d" % k, "e%d" % P
+        for ci, ch in enumerate(CHUNKS):
+            G["c"], G["k"] = str(ci), k
+            v0, v1 = ch["c"]
             w0, w1 = v0 // 16, v1 // 16
+            w = w1 - w0
             we = M if ci == 0 else W
-            subs = [(x, x + sub) for x in range(v0, v1, sub)]
-            eps = "ps%d" % ci
+            eps = EPS[ci]
             L = lambda nm: ("%s%d" % (nm, P), w0, w1)
+            H = lambda j: (eps, 128 * j, 128 * j + w)
+            S = lambda st: cut(ch[st], v0)
             nf = ("nf%d" % k, w0, w1)
-            for x, y in subs:
-                gat("a" if ci or x == v0 else "v", ("hb%d" % P, x, y), (Nk, 0, we), ("n16_%d" % k, x // 16, y // 16))
-            ext(eps, "zn", "hb%d" % P, v0, v1)
-            tc(L("h16_"), (eps, 0, w1 - w0))
-            tt(L("dh"), (eps, 0, w1 - w0), nf, A.subtract)
-            for x, y in subs:
-                a0, a1 = own(x, y)
-                ts(("ah%d" % P, x, y), (Qk, a0, a1), -0.5 * 2 ** k, A.add, fast=True)
-                if ci == 0:
-                    ps = "ps%d" % (3 + (x - v0) // sub)
+            ah = ("af%d" if ch["ah"][0] == "a" else "ah%d") % P
+            if ci == 0 and k == 0:
+                for x, y, q in S("hb"):
+                    gtt(("hbh", x, y), ("lw", 0, M // 16), ("hi16", x // 16, y // 16), ("mask", x, y), A.mult)
+                ext(eps, "zh", "hbh", v0, v1)
+            else:
+                for x, y, q in S("hb"):
+                    gat(q, ("hb%d" % P, x, y), (Nk, 0, we), ("n16_%d" % k, x // 16, y // 16))
+                ext(eps, "zn", "hb%d" % P, v0, v1)
+            tc(L("h16_"), H(0))
+            tt(L("dh"), H(0), nf, A.subtract)
+            for x, y, q in S("ah"):
+                if q == "v":
+                    ts((ah, x, y), (Qk,) + own(x, y), -0.5 * 2 ** k, A.add, fast=True)
                 else:
-                    ps = "ps%d" % (5 + sb[0] % 3)
-                    sb[0] += 1
-                mm((ps, 0, y - x), ("am2", 0, 128), (Qk, a0, a1), True, False)
-                gtt(("e%d" % P, x, y), (Qk, 0, we), ("h16_%d" % P, x // 16, y // 16), ("ah%d" % P, x, y), A.subtract)
-                mm((ps, 0, y - x), ("am", 0, 128), ("e%d" % P, x, y), False, True)
-                act(("bits%d" % P, x, y), (ps, 0, y - x), F.Sign, bias=("bias", k, k + 1))
+                    act((ah, x, y), (Qk,) + own(x, y), F.Identity, bias=-0.5 * 2 ** k)
+            for x, y, q in S("e"):
+                h16 = ("h16_%d" % P, x // 16, y // 16)
+                parts = [(bank(), x2, y2) for x2, y2 in halves(x, y)]
+                for ps, x2, y2 in parts:
+                    mm((ps, 0, y2 - x2), ("am2" if q == "v" else "am", 0, 128), (Qk,) + own(x2, y2), True, False)
+                if q == "v":
+                    gtt((e, x, y), (Qk, 0, we), h16, (ah, x, y), A.subtract)
+                else:
+                    gat("a", (e, x, y), (Qk, 0, we), h16)
+                for ps, x2, y2 in parts:
+                    mm((ps, 0, y2 - x2), ("am", 0, 128), (e, x2, y2), False, True)
+                    act(("bits%d" % P, x2, y2), (ps, 0, y2 - x2), F.Sign, bias=("bias" if q == "v" else "biasd", k, k + 1))
             ext(eps, "zc", "bits%d" % P, v0, v1)
-            ts(L("c16_"), (eps, 0, w1 - w0), 0.5, A.mult, 2047.5, A.add)
-            for x, y in subs:
-                act(("ae%d" % P, x, y), ("e%d" % P, x, y), F.Abs, scale=float(2.0 ** -k), bias=-0.5)
-            for x, y in subs:
+            ts(L("c16_"), H(0), 0.5, A.mult, 2047.5, A.add)
+            for x, y, q in S("e"):
+                if q == "v":
+                    act(("ae%d" % P, x, y), (e, x, y), F.Abs, scale=float(2.0 ** -k), bias=-0.5)
+                    continue
+                for x2, y2 in halves(x, y):
+                    ps = bank()
+                    mm((ps, 0, y2 - x2), ("idn", 0, 128), (Qk,) + own(x2, y2), True, False)
+                    mm((ps, 0, y2 - x2), ("idp", 0, 128), (e, x2, y2), False, True)
+                    act(("ae%d" % P, x2, y2), (ps, 0, y2 - x2), F.Abs, scale=float(2.0 ** -k))
+            for x, y, q in S("ok"):
                 gtt(("okb%d" % P, x, y), ("clrs", 0, 4096), ("c16_%d" % P, x // 16, y // 16), ("ae%d" % P, x, y), A.is_ge)
             ext(eps, "z", "okb%d" % P, v0, v1)
-            ts(L("okm"), (eps, 0, w1 - w0), 15.5, A.is_ge)
-            tt(L("t"), L("okm"), L("dn"), A.mult)
-            l3, l4 = ("l34_%d" % P, 2 * w0, w0 + w1), ("l34_%d" % P, w0 + w1, 2 * w1)
-            tt(l3, nf, L("t"), A.subtract)
+            ts(H(1), H(0), 15.5, A.is_ge)
+            tt(H(2), H(1), L("dn"), A.mult)
+            l3, l4, l16 = ("l34_%d" % P, 2 * w0, w0 + w1), ("l34_%d" % P, w0 + w1, 2 * w1), "l16_%d" % P
             if k < RO - 1:
-                tt(l4, ("own", w0, w1), L("t"), A.add)
-                tc(("l16_%d" % P, 2 * w0, 2 * w1), ("l34_%d" % P, 2 * w0, 2 * w1))
-                for x, y in subs:
-                    a0, a1 = own(x, y)
+                tt(l4, H(2), ("own", w0, w1), A.add)
+                tc((l16, w0 + w1, 2 * w1), l4)
+                for x, y, q in S("nw"):
                     o = w0 + w1 + (x - v0) // 16
-                    gat("a", ("nw%d" % (k + 1), a0, a1), (Nk, 0, we), ("l16_%d" % P, o, o + (y - x) // 16))
+                    gat(q, ("nw%d" % (k + 1),) + own(x, y), (Nk, 0, we), (l16, o, o + (y - x) // 16))
                 if ci == 0:
-                    share("nw%d" % (k + 1), "an%d" % (k + 1), 3000.0)
-            else:
-                tc(("l16_%d" % P, 2 * w0, w0 + w1), l3)
-            for x, y in subs:
+                    share("nw%d" % (k + 1), "an%d" % (k + 1), own(0, B), B)
+            tt(l3, nf, H(2), A.subtract)
+            tc((l16, 2 * w0, w0 + w1), l3)
+            for x, y, q in S("up"):
                 a0, a1 = own(x, y)
                 o = 2 * w0 + (x - v0) // 16
-                gtt((Qn, a0, a1), (Qk, 0, we), ("l16_%d" % P, o, o + (y - x) // 16), ("ah%d" % P, x, y), A.add)
+                gtt((Qn, a0, a1), (Qk, 0, we), (l16, o, o + (y - x) // 16), (ah, x, y), A.add)
                 if k == RO - 1:
-                    if y < v1:
-                        act(("yout", x, y), (Qn, a0, a1), F.Identity, scale=float(2.0 ** -RO), bias=-128.0)
-                    else:
-                        ts(("yout", x, y), (Qn, a0, a1), 2.0 ** -RO, A.mult, -128.0, A.add, fast=True)
-            if k == RO - 1:
-                store(T.yq[:, v0:v1], ("yout", v0, v1))
-            elif ci == 0:
-                share(Qn, "aq%d" % (k + 1), 3000.0)
-            tt(L("t2"), L("okm"), L("dh"), A.mult)
-            tt(("nf%d" % (k + 1), w0, w1), nf, L("t2"), A.add)
+                    h = (x + y) // 2
+                    act(("yout", x, h), (Qn, a0, a0 + h - x), F.Identity, scale=float(2.0 ** -RO), bias=-128.0)
+                    ts(("yout", h, y), (Qn, a0 + h - x, a1), 2.0 ** -RO, A.mult, -128.0, A.add, fast=True)
+                    store(T.yq[:, x:y], ("yout", x, y))
+            if k < RO - 1 and ci == 0:
+                share(Qn, "aq%d" % (k + 1), own(0, B), B)
+            tt(H(3), H(1), L("dh"), A.mult)
+            tt(("nf%d" % (k + 1), w0, w1), H(3), nf, A.add)
             if k < RO - 1:
                 tc(("n16_%d" % (k + 1), w0, w1), ("nf%d" % (k + 1), w0, w1))
-                tt(("dn%d" % (1 - P), w0, w1), ("nf%d" % (k + 1), w0, w1), ("own", w0, w1), A.subtract)
+                tt(("dn%d" % (1 - P), w0, w1), H(3), L("dn"), A.add)
             else:
                 store(T.yp[:, w0:w1], ("nf%d" % RO, w0, w1))
     return G, nloc[0]
@@ -352,7 +429,10 @@ def rank_program(g, core, T, topo):
         return
     G, nloc = build(g, core, T, topo)
     ops = G["ops"]
-    start, fin = schedule(ops)
+    order = schedule(ops)
+    pos = [0] * len(ops)
+    for j, i in enumerate(order):
+        pos[i] = j
     eng = {"v": g.vector, "a": g.scalar, "p": g.tensor, "g": g, "s": g.sync}
     cnt = {"v": 0, "a": 0, "p": 0, "g": 0}
     known = {q: {} for q in eng}
@@ -367,14 +447,14 @@ def rank_program(g, core, T, topo):
         for a, b in snap[d].items():
             if k.get(a, 0) < b:
                 k[a] = b
-    for i in sorted(range(len(ops)), key=lambda i: (start[i], i)):
+    for i in order:
         o = ops[i]
         q = o["q"]
         if o["kind"] == "n":
             tok[i] = (o["sem"], o["val"])
             snap[i] = {o["sem"]: o["val"]}
             continue
-        for d in sorted(o["edges"], key=lambda d: -fin[d]):
+        for d in sorted(o["edges"], key=lambda d: -pos[d]):
             if q == "p" and ops[d]["q"] == "p" and not o["edges"][d]:
                 continue
             if ops[d]["kind"] != "s":

from concourse.bass import DstId, RemoteDMATransfer
from concourse.mybir import AluOpType, ActivationFunctionType

N, V, B, RO = 4, 2048, 512, 5
M = N * B
W = M + V - B

CHUNKS = [
    {"c": (0, 512), "hb": "a256 v256", "e": "v256 a256", "ah": "a512", "ok": "v512", "nw": "a256 v256", "up": "v512"},
    {"c": (512, 1280), "hb": "a768", "e": "v768", "ah": "v768", "ok": "v768", "nw": "a768", "up": "v768"},
    {"c": (1280, 2048), "hb": "a256 a256 v256", "e": "a384 v384", "ah": "v768", "ok": "v768", "nw": "a384 a384", "up": "v384 v384"},
]
EPS = ["ps0", "ps1", "ps2"]
SUMS = ["ps3", "ps4", "ps5", "ps6", "ps7"]

SCRATCH = {}
_BF, _FH, _F32, _I32, _U16 = "bfloat16", "float16", "float32", "int32", "uint16"
for _nm, _n, _d in (
        [(x, 128, _I32) for x in ("parI", "hiI", "loI", "lw")] + [(x, 128, _BF) for x in ("hib", "lob", "am", "am2", "idp", "idn")]
        + [(x, V, _BF) for x in ("qraw", "yout")] + [("clrs", 4096, _BF), ("ones", 16, _BF), ("yb", 16 + 2048, _BF)]
        + [(x, 144, _BF) for x in ("z", "zn", "zc")] + [("zh", 144, _FH)] + [(x, 1, _I32) for x in ("thI", "pI", "pmI")]
        + [(x, 1, _F32) for x in ("thf", "thr", "thd", "pm", "pd", "wn")] + [(x, 8, _F32) for x in ("bias", "biasd", "rowg")]
        + [(x, 16, _F32) for x in ("row", "oh", "pw", "pwo")] + [(x, 128, _F32) for x in ("own0", "own", "rowp")]
        + [("hbh", B, _FH), ("mask", B, _BF), ("lo16", 32, _U16), ("hi16", 32, _U16)]
        + [("Q%d" % k, W, _BF) for k in range(RO + 1)] + [("nf%d" % k, 128, _F32) for k in range(RO + 1)]
        + [("nw%d" % k, W, _BF) for k in range(RO)] + [("n16_%d" % k, 128, _U16) for k in range(RO)]
        + [("%s%d" % (x, k), V, _BF) for k in range(2) for x in ("hb", "bits", "okb", "e", "ae")]
        + [("ah%d" % k, V, _FH) for k in range(2)] + [("af%d" % k, V, _F32) for k in range(2)]
        + [("%s%d" % (x, k), 128, _F32) for k in range(2) for x in ("dn", "dh")]
        + [("%s%d" % (x, k), 128, _U16) for k in range(2) for x in ("h16_", "c16_")]
        + [("l34_%d" % k, 256, _F32) for k in range(2)] + [("l16_%d" % k, 256, _U16) for k in range(2)]):
    SCRATCH[_nm] = ("sbuf", [128, _n], _d)
for _k in range(8):
    SCRATCH["ps%d" % _k] = ("psum", [128, 512], "float32")
SEMAPHORES = ["sv", "sa", "sp", "sg", "ls", "al"] + ["%s%d" % (x, k) for x in ("an", "aq") for k in range(RO)] \
    + ["%s%d" % (x, k) for x in ("ld", "st") for k in range(12)]
QSEM = {"v": "sv", "a": "sa", "p": "sp", "g": "sg"}

FAC, GEL, PE, WAKE, SAME, ISSUE, FLIGHT, DMA = 1.15, 1.56, 0.5, 90.0, 30.0, 700.0, 3000.0, 2000.0
LEAD = {"0 gat hb": -20249, "i ts Q": -9028, "k0 c0": -2637, "0 act yout": -2259, "k0 c2": -3217, "0 tt dh": 24050, "0 act ae": -1574,
        "2 gat hb": 1436, "0 gtt Q": -2179, "2 tc n16_": -5807, "i ms pw": -18957, "i ts thr": -4266, "0 tc h16_": 2660,
        "1 tt l34_": 8487, "1 ts ah": -17644, "1 tc l16_": 10989, "k4 c2": -7641, "1 gat hb": -7582, "2 gtt Q": -1943, "k4 c0": -1459}


def cost(kind, q, c):
    if kind == "d":
        return DMA + c[0]
    if kind == "s":
        return ISSUE
    if kind == "n":
        return FLIGHT
    return FAC * (PE * c[1] if q == "p" else c[0] + 0.83 * (c[1] + GEL * c[2]))


def add(G, q, c, reads, writes, fn, kind="c", sem=None, val=0, deps=(), tag=""):
    i = len(G["ops"])
    edges = {d: True for d in deps}
    for kindrw, regs in ((0, reads), (1, writes)):
        for (nm, c0, c1) in regs:
            psum = nm[:2] == "ps"
            for (a0, a1, o, w) in G["hist"].setdefault(nm, []):
                other = psum and G["ops"][o]["q"] != q
                if not other and (a0 >= c1 or c0 >= a1):
                    continue
                if w and not kindrw:
                    edges[o] = True
                elif kindrw or other:
                    edges.setdefault(o, False)
    for kindrw, regs in ((0, reads), (1, writes)):
        for (nm, c0, c1) in regs:
            h = G["hist"][nm]
            psum = nm[:2] == "ps"
            if kindrw:
                h[:] = [x for x in h if not ((psum and q == "p") or (x[0] >= c0 and x[1] <= c1 and (
                    not psum or x[2] == i or G["ops"][x[2]]["q"] == q)))]
            h.append((c0, c1, i, kindrw))
    lead = LEAD.get("%s %s" % (G["c"], tag), 0.0) + LEAD.get("k%d c%s" % (G["k"], G["c"]), 0.0)
    G["ops"].append({"q": q, "cost": cost(kind, q, c), "fn": fn, "kind": kind, "sem": sem, "val": val, "edges": edges, "lead": lead})
    return i


def schedule(ops):
    n = len(ops)
    succ = [[] for _ in range(n)]
    for i, o in enumerate(ops):
        for d in o["edges"]:
            succ[d].append(i)
    step = lambda a, b: WAKE if ops[a]["q"] != ops[b]["q"] else SAME
    way = [0.0] * n
    for i in range(n - 1, -1, -1):
        way[i] = ops[i]["cost"] + max([way[s] + step(i, s) for s in succ[i]] or [0.0])
    pri = [w + o["lead"] for w, o in zip(way, ops)]
    left = [len(o["edges"]) for o in ops]
    ready, free = {}, {}
    rt, start = [0.0] * n, [0.0] * n
    for i in range(n):
        if left[i] == 0:
            ready.setdefault(ops[i]["q"], []).append(i)
    for _ in range(n):
        best = None
        for q in sorted(ready):
            lst = ready[q]
            if not lst:
                continue
            first = min(rt[i] for i in lst)
            s = first if q == "n" else max(free.get(q, 0.0), first)
            if best is None or s < best[0]:
                best = (s, q, max((i for i in lst if rt[i] <= s + 1e-9), key=lambda i: pri[i]))
        s, q, c = best
        ready[q].remove(c)
        start[c] = s
        f = s + ops[c]["cost"]
        free[q] = s + 60.0 if ops[c]["kind"] == "d" else f
        for x in succ[c]:
            rt[x] = max(rt[x], f + step(c, x))
            left[x] -= 1
            if left[x] == 0:
                ready.setdefault(ops[x]["q"], []).append(x)
    return sorted(range(n), key=lambda i: (start[i], i))


def build(g, core, T, topo):
    A, F = AluOpType, ActivationFunctionType
    r = T.rank_of(core)
    G = {"ops": [], "hist": {}, "c": "i", "k": -1}
    X = lambda nm, a, b, s=1: T[nm][:, a:b] if s == 1 else T[nm][:, a:b:s]
    Y = lambda s: X(*s) if isinstance(s, tuple) else s
    bare = lambda nm: nm.rstrip("0123456789")

    def ts(out, in0, s1, op0, s2=None, op1=None, fast=False):
        def fn():
            if op1 is None:
                return g.vector.tensor_scalar(X(*out), X(*in0), Y(s1), None, op0)
            return g.vector.tensor_scalar(X(*out), X(*in0), Y(s1), Y(s2), op0, op1)
        rd = [in0] + [s for s in (s1, s2) if isinstance(s, tuple)]
        cyc = max(64.0, (in0[2] - in0[1]) * (0.5 if fast else 1.0))
        return add(G, "v", (0, cyc, 0), rd, [out[:3]], fn, tag="ts " + bare(out[0]))

    def tt(out, in0, in1, op):
        cyc = max(64.0, (in0[2] - in0[1]) * (1.0 if "ps" in (in0[0][:2], in1[0][:2]) else 2.0))
        return add(G, "v", (0, cyc, 0), [in0, in1], [out],
                   lambda: g.vector.tensor_tensor(X(*out), X(*in0), X(*in1), op), tag="tt " + bare(out[0]))

    def tc(out, in0):
        return add(G, "v", (0, max(64.0, in0[2] - in0[1]), 0), [in0], [out],
                   lambda: g.vector.tensor_copy(X(*out), X(*in0)), tag="tc " + bare(out[0]))

    def ms(out, val):
        return add(G, "v", (0, 64, 0), [], [out], lambda: g.vector.memset(X(*out), val), tag="ms " + bare(out[0]))

    def act(out, in0, func, **kw):
        rd = [in0] + [v for v in kw.values() if isinstance(v, tuple)]
        return add(G, "a", (40, max(64.0, in0[2] - in0[1]), 0), rd, [out],
                   lambda: g.scalar.activation(X(*out), X(*in0), func, **{nm: Y(v) for nm, v in kw.items()}),
                   tag="act " + bare(out[0]))

    def gat(q, out, win, off):
        def fn():
            w = X(*win).indirect(X(*off))
            return g.vector.tensor_copy(X(*out), w) if q == "v" else g.scalar.activation(X(*out), w, F.Copy)
        return add(G, q, (50 if q == "v" else 65, 0, out[2] - out[1]), [win, off], [out], fn, tag="gat " + bare(out[0]))

    def gtt(out, win, off, in1, op):
        return add(G, "v", (50, 0, out[2] - out[1]), [win, off, in1], [out],
                   lambda: g.vector.tensor_tensor(X(*out), X(*win).indirect(X(*off)), X(*in1), op), tag="gtt " + bare(out[0]))

    def mm(outs, lhs, rhs, start, stop):
        return add(G, "p", (0, max(64, rhs[2] - rhs[1]), 0), [lhs, rhs], [outs],
                   lambda: g.tensor.matmul(X(*outs), X(*lhs), X(*rhs), start, stop), tag="mm")

    def ext(ps, zname, src, v0, v1):
        w = (v1 - v0) // 16

        def fn():
            for i in range(16):
                ins = g.tensor.matmul(T[ps][:, 0:w], T[zname][:, 15 - i:143 - i], T[src][:, v0 + i:v1:16], i == 0, i == 15)
            return ins
        return add(G, "p", (0, 16 * max(64, w), 0), [(zname, 0, 144), (src, v0, v1)], [(ps, 0, w)], fn, tag="ext " + bare(src))

    def spread(ps, c0):
        def fn():
            for i in range(16):
                o = T[ps][:, i:512:16]
                g.tensor.matmul(o, T["yb"][:, 16 + 128 * i:144 + 128 * i], T["hib"][:, c0:c0 + 32], True, False)
                ins = g.tensor.matmul(o, T["yb"][:, 15 + 128 * i:143 + 128 * i], T["lob"][:, c0:c0 + 32], False, True)
            return ins
        return add(G, "p", (0, 32 * 64, 0), [("yb", 0, 2064), ("hib", c0, c0 + 32), ("lob", c0, c0 + 32)], [(ps, 0, 512)], fn,
                   tag="spread")

    nst = [0]

    def load(q, k, out, src, more=0.0):
        eng = g.sync if q == "s" else g.scalar
        return add(G, q, (more,), [], [out], lambda: eng.dma_start(X(*out), src), "d", "ld%d" % k, 16, tag="load")

    def store(dst, src):
        k = nst[0]
        nst[0] += 1
        return add(G, "s", (0.0,), [src], [], lambda: g.sync.dma_start(dst, X(*src)), "d", "st%d" % k, 16, tag="store")

    peers = [c for c in T.cores if c != core]
    near = [c for c in peers if topo.chip(c) == topo.chip(core)]
    far = [c for c in peers if topo.chip(c) != topo.chip(core)]
    efar = [e for e in topo.engines(core, far[0]) if all(e in topo.engines(core, c) for c in far)]
    enear = [e for e in topo.engines(core, near[0]) if e not in efar]
    nloc = [0]

    def share(buf, sem, cols, step):
        c0, c1 = cols

        def fn():
            tr = []
            for dsts, eng in ((far, efar), (near, enear)):
                ids = []
                for c in dsts:
                    rid, pid, se = topo.addr(c)
                    ids.append(DstId(rid=rid, pnc=pid))
                tr.append(RemoteDMATransfer(dst_ids=ids, dma_engine_mask=sum(1 << e for e in eng), remote_sem=T.sem[sem],
                                            srcs=[X(buf, c0, c1)], dsts=[X(buf, c0, c1)] * len(ids)))
            return g.remote_dma_fused(tr, local_sem=T.sem.ls)
        nloc[0] += len(efar) + len(enear)
        i = add(G, "g", (0.0,), [(buf, c0, c1)], [], fn, "s", tag="share " + bare(buf))
        tot = 0
        for c in peers:
            f2 = [x for x in T.cores if topo.chip(x) != topo.chip(c)]
            e2 = topo.engines(c, f2[0])
            tot += len(e2) if topo.chip(c) != topo.chip(core) else len([e for e in topo.engines(c, core) if e not in e2])
        wr = [(buf, a, b) for (a, b) in ((0, c0), (c1, N * step)) if b > a]
        add(G, "n", (0.0,), [], wr, None, "n", sem, tot, deps=[i], tag="arr " + bare(buf))

    def own(v0, v1):
        o = r * B if v1 <= B else M - B
        return (v0 + o, v1 + o)

    mine = ("lw", 32 * r, 32 * r + 32)
    load("s", 0, mine, T.par[:, 0:32])
    load("a", 1, ("qraw", 0, B), T.q[:, 0:B])
    load("s", 2, ("parI", 32, 128), T.par[:, 32:128])
    load("s", 3, ("am", 0, 128), T.amat[:, :])
    load("s", 4, ("thI", 0, 1), T.th[:, :])
    load("s", 5, ("qraw", B, V), T.q[:, B:V], 1000.0)
    load("s", 6, ("clrs", 0, 4096), T.clr[:, :], 3000.0)

    def io(out, pattern, base, cm, flag):
        kw = {"allow_small_or_imprecise_dtypes": True} if flag else {}
        return add(G, "g", (130, 2 * (out[2] - out[1]), 0), [], [out], lambda: g.iota(X(*out), pattern, base, cm, **kw), tag="iota")
    io(("pI", 0, 1), [[0, 1]], 0, 1, False)
    io(("rowg", 0, 8), [[16, 8]], 0, 0, True)
    io(("row", 0, 16), [[1, 16]], 0, 0, True)
    io(("own0", 0, 32), [[16, 32]], r * B, 0, True)
    io(("own0", 32, 128), [[16, 96]], M, 0, True)
    io(("rowp", 0, 128), [[1, 128]], 0, -1, True)
    ts(("pmI", 0, 1), ("pI", 0, 1), 15, A.bitwise_and)
    tc(("pm", 0, 1), ("pmI", 0, 1))
    tt(("pd", 0, 1), ("pI", 0, 1), ("pm", 0, 1), A.subtract)
    ts(("oh", 0, 16), ("row", 0, 16), ("pm", 0, 1), A.is_equal)
    ms(("z", 0, 144), 0.0)
    ts(("z", 15, 128, 16), ("rowg", 0, 8), ("pd", 0, 1), A.is_equal)
    tc(("zh", 0, 144), ("z", 0, 144))
    ms(("yb", 0, 16), 0.0)
    for i in range(16):
        ts(("yb", 16 + 128 * i, 144 + 128 * i), ("z", 15, 143), ("oh", i, i + 1), A.mult, fast=True)

    def names0(c0, c1):
        src = mine if c0 == 0 else ("parI", c0, c1)
        ts(("hiI", c0, c1), src, 4, A.arith_shift_right)
        ts(("loI", c0, c1), src, 15, A.bitwise_and)
        tc(("hib", c0, c1), ("hiI", c0, c1))
        tc(("lob", c0, c1), ("loI", c0, c1))
        if c0 == 0:
            tc(("lo16", 0, 32), ("loI", 0, 32))
            tc(("hi16", 0, 32), ("hiI", 0, 32))
            for x in (0, 256):
                gat("a" if x else "v", ("mask", x, x + 256), ("oh", 0, 16), ("lo16", x // 16, x // 16 + 16))
        for b in range(c0, c1, 32):
            ps = "ps%d" % (3 + (b // 32))
            spread(ps, b)
            a0, a1 = own(16 * b, 16 * b + 512)
            act(("nw0", a0, a0 + 256), (ps, 0, 256), F.Copy)
            if b == 0:
                tc(("nw0", a0 + 256, a1), (ps, 256, 512))
            else:
                act(("nw0", a0 + 256, a1), (ps, 256, 512), F.Copy)
    share("lw", "al", mine[1:], 32)
    a0, a1 = own(0, B)
    ts(("Q0", a0, a1), ("qraw", 0, B), 128.0, A.add, fast=True)
    share("Q0", "aq0", own(0, B), B)
    names0(0, 32)
    share("nw0", "an0", own(0, B), B)
    ts(("wn", 0, 1), ("oh", 0, 1), 16.0, A.mult, ("oh", 1, 2), A.add)
    ms(("pw", 12, 16), 0.0)
    for i in range(12):
        ms(("pw", i, i + 1), float(2 ** i))
    tt(("pwo", 0, 16), ("pw", 0, 16), ("oh", 0, 16), A.mult)
    for h in (8, 4, 2, 1):
        tt(("pwo", 0, h), ("pwo", 0, h), ("pwo", h, 2 * h), A.add)
    ts(("zn", 0, 144), ("z", 0, 144), ("wn", 0, 1), A.mult, fast=True)
    ts(("zc", 0, 144), ("z", 0, 144), ("pwo", 0, 1), A.mult, fast=True)
    ts(("own", 0, 128), ("own0", 0, 128), ("pm", 0, 1), A.add)
    ts(("idp", 0, 128), ("rowp", 0, 128), 0.0, A.is_equal)
    ts(("idn", 0, 128), ("idp", 0, 128), -1.0, A.mult, fast=True)
    for (c0, c1) in ((0, 32), (32, 128)):
        src = mine if c0 == 0 else ("parI", c0, c1)
        tc(("nf0", c0, c1), src)
        tc(("n16_0", c0, c1), src)
        tt(("dn0", c0, c1), ("nf0", c0, c1), ("own", c0, c1), A.subtract)
    ms(("ones", 0, 16), 1.0)
    mm(("ps7", 0, 2), ("am", 0, 128), ("ones", 0, 2), True, True)
    tc(("thf", 0, 1), ("thI", 0, 1))
    ts(("thr", 0, 1), ("ps7", 0, 1), 256.5, A.mult, ("thf", 0, 1), A.add)
    ts(("thd", 0, 1), ("ps7", 0, 1), 256.0, A.mult, ("thf", 0, 1), A.add)
    for k in range(RO):
        ts(("bias", k, k + 1), ("thr", 0, 1), 0.5, A.add, -float(2 ** k), A.mult)
        ts(("biasd", k, k + 1), ("thd", 0, 1), 0.5, A.add, -float(2 ** k), A.mult)
    ts(("am2", 0, 128), ("am", 0, 128), 2.0, A.mult, fast=True)
    names0(32, 128)
    a0, a1 = own(B, V)
    ts(("Q0", a0, a1), ("qraw", B, V), 128.0, A.add, fast=True)

    sb = [0]

    def bank():
        sb[0] += 1
        return SUMS[(sb[0] - 1) % len(SUMS)]

    def cut(text, x):
        out = []
        for t in text.split():
            out.append((x, x + int(t[1:]), t[0]))
            x = out[-1][1]
        return out

    def halves(x, y):
        m = -(-(y - x) // 512)
        return [(x + (y - x) * j // m, x + (y - x) * (j + 1) // m) for j in range(m)]

    for k in range(RO):
        P = k % 2
        Qk, Qn, Nk, e = "Q%d" % k, "Q%d" % (k + 1), "nw%d" % k, "e%d" % P
        for ci, ch in enumerate(CHUNKS):
            G["c"], G["k"] = str(ci), k
            v0, v1 = ch["c"]
            w0, w1 = v0 // 16, v1 // 16
            w = w1 - w0
            we = M if ci == 0 else W
            eps = EPS[ci]
            L = lambda nm: ("%s%d" % (nm, P), w0, w1)
            H = lambda j: (eps, 128 * j, 128 * j + w)
            S = lambda st: cut(ch[st], v0)
            nf = ("nf%d" % k, w0, w1)
            ah = ("af%d" if ch["ah"][0] == "a" else "ah%d") % P
            if ci == 0 and k == 0:
                for x, y, q in S("hb"):
                    gtt(("hbh", x, y), ("lw", 0, M // 16), ("hi16", x // 16, y // 16), ("mask", x, y), A.mult)
                ext(eps, "zh", "hbh", v0, v1)
            else:
                for x, y, q in S("hb"):
                    gat(q, ("hb%d" % P, x, y), (Nk, 0, we), ("n16_%d" % k, x // 16, y // 16))
                ext(eps, "zn", "hb%d" % P, v0, v1)
            tc(L("h16_"), H(0))
            tt(L("dh"), H(0), nf, A.subtract)
            for x, y, q in S("ah"):
                if q == "v":
                    ts((ah, x, y), (Qk,) + own(x, y), -0.5 * 2 ** k, A.add, fast=True)
                else:
                    act((ah, x, y), (Qk,) + own(x, y), F.Identity, bias=-0.5 * 2 ** k)
            for x, y, q in S("e"):
                h16 = ("h16_%d" % P, x // 16, y // 16)
                parts = [(bank(), x2, y2) for x2, y2 in halves(x, y)]
                for ps, x2, y2 in parts:
                    mm((ps, 0, y2 - x2), ("am2" if q == "v" else "am", 0, 128), (Qk,) + own(x2, y2), True, False)
                if q == "v":
                    gtt((e, x, y), (Qk, 0, we), h16, (ah, x, y), A.subtract)
                else:
                    gat("a", (e, x, y), (Qk, 0, we), h16)
                for ps, x2, y2 in parts:
                    mm((ps, 0, y2 - x2), ("am", 0, 128), (e, x2, y2), False, True)
                    act(("bits%d" % P, x2, y2), (ps, 0, y2 - x2), F.Sign, bias=("bias" if q == "v" else "biasd", k, k + 1))
            ext(eps, "zc", "bits%d" % P, v0, v1)
            ts(L("c16_"), H(0), 0.5, A.mult, 2047.5, A.add)
            for x, y, q in S("e"):
                if q == "v":
                    act(("ae%d" % P, x, y), (e, x, y), F.Abs, scale=float(2.0 ** -k), bias=-0.5)
                    continue
                for x2, y2 in halves(x, y):
                    ps = bank()
                    mm((ps, 0, y2 - x2), ("idn", 0, 128), (Qk,) + own(x2, y2), True, False)
                    mm((ps, 0, y2 - x2), ("idp", 0, 128), (e, x2, y2), False, True)
                    act(("ae%d" % P, x2, y2), (ps, 0, y2 - x2), F.Abs, scale=float(2.0 ** -k))
            for x, y, q in S("ok"):
                gtt(("okb%d" % P, x, y), ("clrs", 0, 4096), ("c16_%d" % P, x // 16, y // 16), ("ae%d" % P, x, y), A.is_ge)
            ext(eps, "z", "okb%d" % P, v0, v1)
            ts(H(1), H(0), 15.5, A.is_ge)
            tt(H(2), H(1), L("dn"), A.mult)
            l3, l4, l16 = ("l34_%d" % P, 2 * w0, w0 + w1), ("l34_%d" % P, w0 + w1, 2 * w1), "l16_%d" % P
            if k < RO - 1:
                tt(l4, H(2), ("own", w0, w1), A.add)
                tc((l16, w0 + w1, 2 * w1), l4)
                for x, y, q in S("nw"):
                    o = w0 + w1 + (x - v0) // 16
                    gat(q, ("nw%d" % (k + 1),) + own(x, y), (Nk, 0, we), (l16, o, o + (y - x) // 16))
                if ci == 0:
                    share("nw%d" % (k + 1), "an%d" % (k + 1), own(0, B), B)
            tt(l3, nf, H(2), A.subtract)
            tc((l16, 2 * w0, w0 + w1), l3)
            for x, y, q in S("up"):
                a0, a1 = own(x, y)
                o = 2 * w0 + (x - v0) // 16
                gtt((Qn, a0, a1), (Qk, 0, we), (l16, o, o + (y - x) // 16), (ah, x, y), A.add)
                if k == RO - 1:
                    h = (x + y) // 2
                    act(("yout", x, h), (Qn, a0, a0 + h - x), F.Identity, scale=float(2.0 ** -RO), bias=-128.0)
                    ts(("yout", h, y), (Qn, a0 + h - x, a1), 2.0 ** -RO, A.mult, -128.0, A.add, fast=True)
                    store(T.yq[:, x:y], ("yout", x, y))
            if k < RO - 1 and ci == 0:
                share(Qn, "aq%d" % (k + 1), own(0, B), B)
            tt(H(3), H(1), L("dh"), A.mult)
            tt(("nf%d" % (k + 1), w0, w1), H(3), nf, A.add)
            if k < RO - 1:
                tc(("n16_%d" % (k + 1), w0, w1), ("nf%d" % (k + 1), w0, w1))
                tt(("dn%d" % (1 - P), w0, w1), H(3), L("dn"), A.add)
            else:
                store(T.yp[:, w0:w1], ("nf%d" % RO, w0, w1))
    return G, nloc[0]


def rank_program(g, core, T, topo):
    if T.rank_of(core) is None:
        return
    G, nloc = build(g, core, T, topo)
    ops = G["ops"]
    order = schedule(ops)
    pos = [0] * len(ops)
    for j, i in enumerate(order):
        pos[i] = j
    eng = {"v": g.vector, "a": g.scalar, "p": g.tensor, "g": g, "s": g.sync}
    cnt = {"v": 0, "a": 0, "p": 0, "g": 0}
    known = {q: {} for q in eng}
    tok, snap = {}, {}

    def wait(q, d):
        s, v = tok[d]
        k = known[q]
        if k.get(s, 0) >= v:
            return
        eng[q].wait_ge(T.sem[s], v)
        for a, b in snap[d].items():
            if k.get(a, 0) < b:
                k[a] = b
    for i in order:
        o = ops[i]
        q = o["q"]
        if o["kind"] == "n":
            tok[i] = (o["sem"], o["val"])
            snap[i] = {o["sem"]: o["val"]}
            continue
        for d in sorted(o["edges"], key=lambda d: -pos[d]):
            if q == "p" and ops[d]["q"] == "p" and not o["edges"][d]:
                continue
            if ops[d]["kind"] != "s":
                wait(q, d)
        ins = o["fn"]()
        if o["kind"] == "c":
            cnt[q] += 1
            tok[i] = (QSEM[q], cnt[q])
            ins.then_inc(T.sem[QSEM[q]], 1)
        elif o["kind"] == "d":
            tok[i] = (o["sem"], o["val"])
            ins.then_inc(T.sem[o["sem"]], 16)
        if o["kind"] != "s":
            snap[i] = dict(known[q])
            snap[i][tok[i][0]] = tok[i][1]
    g.wait_ge(T.sem.ls, nloc)
    for i in range(len(ops)):
        if ops[i]["kind"] in ("d", "n"):
            wait("s", i)
    for q in cnt:
        if known["s"].get(QSEM[q], 0) < cnt[q]:
            g.sync.wait_ge(T.sem[QSEM[q]], cnt[q])
